import numpy as np
import ml_dtypes

BF16 = ml_dtypes.bfloat16


def bf(x):
    return np.asarray(x, np.float32).astype(BF16)


def f32(x):
    return np.asarray(x, np.float32)


def f64(x):
    return np.asarray(x).astype(np.float64)


def striped(idx):
    return np.tile(idx.reshape(-1, 16).T, (8, 1))


S, K, M, N = 512, 512, 256, 512


def setup_inputs():
    return {"base": bf(np.random.standard_normal((M, S))), "x": bf(np.random.standard_normal((K, N))), "w": bf(np.random.standard_normal((K, M)) / np.sqrt(K)), "b": f32(0.5 * np.random.standard_normal((M, 1))), "offs": striped(np.random.permutation(S))}


def reference(base, x, w, b, offs):
    idx = offs[:16].T.reshape(-1)
    z = f64(base).copy()
    z[:, idx] += f64(w).T @ f64(x)
    return np.tanh(z + f64(b))

@@ -1,0 +1,52 @@
+import concourse.mybir as mybir
+from concourse.masks import make_identity
+
+P = 128
+S, K, M, N = 512, 512, 256, 512
+KB = K // P
+MB = M // P
+FLOPS = 2 * K * M * N
+
+BF16, F32, U16 = mybir.dt.bfloat16, mybir.dt.float32, mybir.dt.uint16
+TANH = mybir.ActivationFunctionType.Tanh
+
+
+def tile_scatter_matmul_kernel(tc, base, x, w, b, offs, out):
+    nc = tc.nc
+    with (
+        tc.tile_pool(name="held", bufs=1) as held,
+        tc.psum_pool(name="banks", bufs=1) as banks,
+    ):
+        offsets = held.tile([P, N // 16], U16, name="offsets")
+        nc.sync.dma_start(offsets[:], offs)
+
+        base_sb = held.tile([P, MB, S], BF16, name="base_sb")
+        nc.scalar.dma_start(base_sb[:], base.rearrange("(a p) s -> p a s", p=P))
+        w_sb = held.tile([P, KB, M], BF16, name="w_sb")
+        nc.scalar.dma_start(w_sb[:], w.rearrange("(k p) m -> p k m", p=P))
+        bias = held.tile([P, MB], F32, name="bias")
+        nc.scalar.dma_start(bias[:], b.rearrange("(a p) o -> p (a o)", p=P))
+
+        x_sb = [held.tile([P, N], BF16, name="x_sb%d" % k) for k in range(KB)]
+        for k in range(KB):
+            nc.sync.dma_start(x_sb[k][:], x[k * P : (k + 1) * P, :])
+
+        ident = held.tile([P, P], BF16, name="ident")
+        make_identity(nc, ident[:])
+
+        window = [banks.tile([P, S], F32, name="window%d" % a) for a in range(MB)]
+        for a in range(MB):
+            nc.tensor.matmul(window[a][:], ident[:], base_sb[:, a, :], start=True, stop=False)
+
+        for a in range(MB):
+            for k in range(KB):
+                nc.tensor.matmul(
+                    window[a][:].indirect(offsets[:]),
+                    w_sb[:, k, a * P : (a + 1) * P],
+                    x_sb[k][:],
+                    start=False,
+                    stop=(k == KB - 1),
+                )
+            result = held.tile([P, S], F32, name="result%d" % a)
+            nc.scalar.activation(result[:], window[a][:], TANH, bias=bias[:, a : a + 1])
+            nc.sync.dma_start(out[a * P : (a + 1) * P, :], result[:])

@@ -5,6 +5,7 @@ P = 128
 S, K, M, N = 512, 512, 256, 512
 KB = K // P
 MB = M // P
+WARM = 16
 FLOPS = 2 * K * M * N
 
 BF16, F32, U16 = mybir.dt.bfloat16, mybir.dt.float32, mybir.dt.uint16
@@ -30,6 +31,12 @@ def tile_scatter_matmul_kernel(tc, base, x, w, b, offs, out):
         x_sb = [held.tile([P, N], BF16, name="x_sb%d" % k) for k in range(KB)]
         for k in range(KB):
             nc.sync.dma_start(x_sb[k][:], x[k * P : (k + 1) * P, :])
+
+        zeros = held.tile([P, P], BF16, name="zeros")
+        nc.gpsimd.memset(zeros[:], 0.0)
+        idle_bank = banks.tile([P, P], F32, name="idle_bank")
+        for i in range(WARM):
+            nc.tensor.matmul(idle_bank[:], zeros[:], zeros[:], start=True, stop=True)
 
         ident = held.tile([P, P], BF16, name="ident")
         make_identity(nc, ident[:])

@@ -6,6 +6,8 @@ S, K, M, N = 512, 512, 256, 512
 KB = K // P
 MB = M // P
 WARM = 16
+W_PIECES = ((0, 2), (2, 4))
+X_PIECES = ((0, 1), (1, 2), (2, 4))
 FLOPS = 2 * K * M * N
 
 BF16, F32, U16 = mybir.dt.bfloat16, mybir.dt.float32, mybir.dt.uint16
@@ -21,16 +23,22 @@ def tile_scatter_matmul_kernel(tc, base, x, w, b, offs, out):
         offsets = held.tile([P, N // 16], U16, name="offsets")
         nc.sync.dma_start(offsets[:], offs)
 
-        base_sb = held.tile([P, MB, S], BF16, name="base_sb")
-        nc.scalar.dma_start(base_sb[:], base.rearrange("(a p) s -> p a s", p=P))
-        w_sb = held.tile([P, KB, M], BF16, name="w_sb")
-        nc.scalar.dma_start(w_sb[:], w.rearrange("(k p) m -> p k m", p=P))
-        bias = held.tile([P, MB], F32, name="bias")
-        nc.scalar.dma_start(bias[:], b.rearrange("(a p) o -> p (a o)", p=P))
+        base_sb = [held.tile([P, S], BF16, name="base_sb%d" % a) for a in range(MB)]
+        nc.scalar.dma_start(base_sb[0][:], base[0:P, :])
+        nc.sync.dma_start(base_sb[1][:], base[P : 2 * P, :])
 
-        x_sb = [held.tile([P, N], BF16, name="x_sb%d" % k) for k in range(KB)]
-        for k in range(KB):
-            nc.sync.dma_start(x_sb[k][:], x[k * P : (k + 1) * P, :])
+        w_sb = {}
+        for k0, k1 in W_PIECES:
+            w_piece = held.tile([P, k1 - k0, M], BF16, name="w_piece%d" % k0)
+            nc.scalar.dma_start(w_piece[:], w[k0 * P : k1 * P, :].rearrange("(k p) m -> p k m", p=P))
+            for k in range(k0, k1):
+                w_sb[k] = w_piece[:, k - k0, :]
+        x_sb = {}
+        for k0, k1 in X_PIECES:
+            x_piece = held.tile([P, k1 - k0, N], BF16, name="x_piece%d" % k0)
+            nc.sync.dma_start(x_piece[:], x[k0 * P : k1 * P, :].rearrange("(k p) n -> p k n", p=P))
+            for k in range(k0, k1):
+                x_sb[k] = x_piece[:, k - k0, :]
 
         zeros = held.tile([P, P], BF16, name="zeros")
         nc.gpsimd.memset(zeros[:], 0.0)
@@ -41,16 +49,19 @@ def tile_scatter_matmul_kernel(tc, base, x, w, b, offs, out):
         ident = held.tile([P, P], BF16, name="ident")
         make_identity(nc, ident[:])
 
+        bias = held.tile([P, MB], F32, name="bias")
+        nc.gpsimd.dma_start(bias[:], b.rearrange("(a p) o -> p (a o)", p=P))
+
         window = [banks.tile([P, S], F32, name="window%d" % a) for a in range(MB)]
         for a in range(MB):
-            nc.tensor.matmul(window[a][:], ident[:], base_sb[:, a, :], start=True, stop=False)
+            nc.tensor.matmul(window[a][:], ident[:], base_sb[a][:], start=True, stop=False)
 
         for a in range(MB):
             for k in range(KB):
                 nc.tensor.matmul(
                     window[a][:].indirect(offsets[:]),
-                    w_sb[:, k, a * P : (a + 1) * P],
-                    x_sb[k][:],
+                    w_sb[k][:, a * P : (a + 1) * P],
+                    x_sb[k],
                     start=False,
                     stop=(k == KB - 1),
                 )

@@ -6,8 +6,7 @@ S, K, M, N = 512, 512, 256, 512
 KB = K // P
 MB = M // P
 WARM = 16
-W_PIECES = ((0, 2), (2, 4))
-X_PIECES = ((0, 1), (1, 2), (2, 4))
+HALF = S // 2
 FLOPS = 2 * K * M * N
 
 BF16, F32, U16 = mybir.dt.bfloat16, mybir.dt.float32, mybir.dt.uint16
@@ -23,22 +22,16 @@ def tile_scatter_matmul_kernel(tc, base, x, w, b, offs, out):
         offsets = held.tile([P, N // 16], U16, name="offsets")
         nc.sync.dma_start(offsets[:], offs)
 
-        base_sb = [held.tile([P, S], BF16, name="base_sb%d" % a) for a in range(MB)]
-        nc.scalar.dma_start(base_sb[0][:], base[0:P, :])
-        nc.sync.dma_start(base_sb[1][:], base[P : 2 * P, :])
+        base_sb = held.tile([P, MB, S], BF16, name="base_sb")
+        nc.scalar.dma_start(base_sb[:], base.rearrange("(a p) s -> p a s", p=P))
+        w_sb = held.tile([P, KB, M], BF16, name="w_sb")
+        nc.scalar.dma_start(w_sb[:], w.rearrange("(k p) m -> p k m", p=P))
+        bias = held.tile([P, MB], F32, name="bias")
+        nc.scalar.dma_start(bias[:], b.rearrange("(a p) o -> p (a o)", p=P))
 
-        w_sb = {}
-        for k0, k1 in W_PIECES:
-            w_piece = held.tile([P, k1 - k0, M], BF16, name="w_piece%d" % k0)
-            nc.scalar.dma_start(w_piece[:], w[k0 * P : k1 * P, :].rearrange("(k p) m -> p k m", p=P))
-            for k in range(k0, k1):
-                w_sb[k] = w_piece[:, k - k0, :]
-        x_sb = {}
-        for k0, k1 in X_PIECES:
-            x_piece = held.tile([P, k1 - k0, N], BF16, name="x_piece%d" % k0)
-            nc.sync.dma_start(x_piece[:], x[k0 * P : k1 * P, :].rearrange("(k p) n -> p k n", p=P))
-            for k in range(k0, k1):
-                x_sb[k] = x_piece[:, k - k0, :]
+        x_sb = [held.tile([P, N], BF16, name="x_sb%d" % k) for k in range(KB)]
+        for k in range(KB):
+            nc.sync.dma_start(x_sb[k][:], x[k * P : (k + 1) * P, :])
 
         zeros = held.tile([P, P], BF16, name="zeros")
         nc.gpsimd.memset(zeros[:], 0.0)
@@ -49,22 +42,21 @@ def tile_scatter_matmul_kernel(tc, base, x, w, b, offs, out):
         ident = held.tile([P, P], BF16, name="ident")
         make_identity(nc, ident[:])
 
-        bias = held.tile([P, MB], F32, name="bias")
-        nc.gpsimd.dma_start(bias[:], b.rearrange("(a p) o -> p (a o)", p=P))
-
         window = [banks.tile([P, S], F32, name="window%d" % a) for a in range(MB)]
         for a in range(MB):
-            nc.tensor.matmul(window[a][:], ident[:], base_sb[a][:], start=True, stop=False)
+            nc.tensor.matmul(window[a][:], ident[:], base_sb[:, a, :], start=True, stop=False)
 
         for a in range(MB):
             for k in range(KB):
                 nc.tensor.matmul(
                     window[a][:].indirect(offsets[:]),
-                    w_sb[k][:, a * P : (a + 1) * P],
-                    x_sb[k],
+                    w_sb[:, k, a * P : (a + 1) * P],
+                    x_sb[k][:],
                     start=False,
                     stop=(k == KB - 1),
                 )
             result = held.tile([P, S], F32, name="result%d" % a)
-            nc.scalar.activation(result[:], window[a][:], TANH, bias=bias[:, a : a + 1])
-            nc.sync.dma_start(out[a * P : (a + 1) * P, :], result[:])
+            for half, queue in enumerate((nc.sync, nc.scalar)):
+                cols = slice(half * HALF, (half + 1) * HALF)
+                nc.scalar.activation(result[:, cols], window[a][:, cols], TANH, bias=bias[:, a : a + 1])
+                queue.dma_start(out[a * P : (a + 1) * P, cols], result[:, cols])

@@ -6,7 +6,6 @@ S, K, M, N = 512, 512, 256, 512
 KB = K // P
 MB = M // P
 WARM = 16
-HALF = S // 2
 FLOPS = 2 * K * M * N
 
 BF16, F32, U16 = mybir.dt.bfloat16, mybir.dt.float32, mybir.dt.uint16
@@ -39,6 +38,9 @@ def tile_scatter_matmul_kernel(tc, base, x, w, b, offs, out):
         for i in range(WARM):
             nc.tensor.matmul(idle_bank[:], zeros[:], zeros[:], start=True, stop=True)
 
+        early_tanh = held.tile([P, 1], F32, name="early_tanh")
+        nc.scalar.activation(early_tanh[:], zeros[:, 0:1], TANH)
+
         ident = held.tile([P, P], BF16, name="ident")
         make_identity(nc, ident[:])
 
@@ -46,17 +48,22 @@ def tile_scatter_matmul_kernel(tc, base, x, w, b, offs, out):
         for a in range(MB):
             nc.tensor.matmul(window[a][:], ident[:], base_sb[:, a, :], start=True, stop=False)
 
+        def scatter_add(a, k):
+            nc.tensor.matmul(
+                window[a][:].indirect(offsets[:]),
+                w_sb[:, k, a * P : (a + 1) * P],
+                x_sb[k][:],
+                start=False,
+                stop=(k == KB - 1),
+            )
+
+        for k in range(KB // 2):
+            for a in range(MB):
+                scatter_add(a, k)
+
         for a in range(MB):
-            for k in range(KB):
-                nc.tensor.matmul(
-                    window[a][:].indirect(offsets[:]),
-                    w_sb[:, k, a * P : (a + 1) * P],
-                    x_sb[k][:],
-                    start=False,
-                    stop=(k == KB - 1),
-                )
+            for k in range(KB // 2, KB):
+                scatter_add(a, k)
             result = held.tile([P, S], F32, name="result%d" % a)
-            for half, queue in enumerate((nc.sync, nc.scalar)):
-                cols = slice(half * HALF, (half + 1) * HALF)
-                nc.scalar.activation(result[:, cols], window[a][:, cols], TANH, bias=bias[:, a : a + 1])
-                queue.dma_start(out[a * P : (a + 1) * P, cols], result[:, cols])
+            nc.scalar.activation(result[:], window[a][:], TANH, bias=bias[:, a : a + 1])
+            nc.sync.dma_start(out[a * P : (a + 1) * P, :], result[:])

@@ -18,19 +18,21 @@ def tile_scatter_matmul_kernel(tc, base, x, w, b, offs, out):
         tc.tile_pool(name="held", bufs=1) as held,
         tc.psum_pool(name="banks", bufs=1) as banks,
     ):
+        base_sb = held.tile([P, MB, S], BF16, name="base_sb")
+        nc.sync.dma_start(base_sb[:], base.rearrange("(a p) s -> p a s", p=P))
+
         offsets = held.tile([P, N // 16], U16, name="offsets")
         nc.sync.dma_start(offsets[:], offs)
 
-        base_sb = held.tile([P, MB, S], BF16, name="base_sb")
-        nc.scalar.dma_start(base_sb[:], base.rearrange("(a p) s -> p a s", p=P))
         w_sb = held.tile([P, KB, M], BF16, name="w_sb")
-        nc.scalar.dma_start(w_sb[:], w.rearrange("(k p) m -> p k m", p=P))
-        bias = held.tile([P, MB], F32, name="bias")
-        nc.scalar.dma_start(bias[:], b.rearrange("(a p) o -> p (a o)", p=P))
+        nc.sync.dma_start(w_sb[:], w.rearrange("(k p) m -> p k m", p=P))
 
         x_sb = [held.tile([P, N], BF16, name="x_sb%d" % k) for k in range(KB)]
         for k in range(KB):
             nc.sync.dma_start(x_sb[k][:], x[k * P : (k + 1) * P, :])
+
+        bias = held.tile([P, MB], F32, name="bias")
+        nc.sync.dma_start(bias[:], b.rearrange("(a p) o -> p (a o)", p=P))
 
         zeros = held.tile([P, P], BF16, name="zeros")
         nc.gpsimd.memset(zeros[:], 0.0)

@@ -6,6 +6,7 @@ S, K, M, N = 512, 512, 256, 512
 KB = K // P
 MB = M // P
 WARM = 16
+CUTS = ((0, 1), (1, 2), (2, KB))
 FLOPS = 2 * K * M * N
 
 BF16, F32, U16 = mybir.dt.bfloat16, mybir.dt.float32, mybir.dt.uint16
@@ -24,12 +25,17 @@ def tile_scatter_matmul_kernel(tc, base, x, w, b, offs, out):
         offsets = held.tile([P, N // 16], U16, name="offsets")
         nc.sync.dma_start(offsets[:], offs)
 
-        w_sb = held.tile([P, KB, M], BF16, name="w_sb")
-        nc.sync.dma_start(w_sb[:], w.rearrange("(k p) m -> p k m", p=P))
-
-        x_sb = [held.tile([P, N], BF16, name="x_sb%d" % k) for k in range(KB)]
-        for k in range(KB):
-            nc.sync.dma_start(x_sb[k][:], x[k * P : (k + 1) * P, :])
+        w_rows = w.rearrange("(p k) m -> p k m", k=KB)
+        x_rows = x.rearrange("(p k) n -> p k n", k=KB)
+        w_block, x_block = {}, {}
+        for first, end in CUTS:
+            w_sb = held.tile([P, end - first, M], BF16, name="w_sb%d" % first)
+            nc.sync.dma_start(w_sb[:], w_rows[:, first:end, :])
+            x_sb = held.tile([P, end - first, N], BF16, name="x_sb%d" % first)
+            nc.sync.dma_start(x_sb[:], x_rows[:, first:end, :])
+            for k in range(first, end):
+                w_block[k] = w_sb[:, k - first, :]
+                x_block[k] = x_sb[:, k - first, :]
 
         bias = held.tile([P, MB], F32, name="bias")
         nc.sync.dma_start(bias[:], b.rearrange("(a p) o -> p (a o)", p=P))
@@ -53,8 +59,8 @@ def tile_scatter_matmul_kernel(tc, base, x, w, b, offs, out):
         def scatter_add(a, k):
             nc.tensor.matmul(
                 window[a][:].indirect(offsets[:]),
-                w_sb[:, k, a * P : (a + 1) * P],
-                x_sb[k][:],
+                w_block[k][:, a * P : (a + 1) * P],
+                x_block[k],
                 start=False,
                 stop=(k == KB - 1),
             )

@@ -5,7 +5,7 @@ P = 128
 S, K, M, N = 512, 512, 256, 512
 KB = K // P
 MB = M // P
-WARM = 16
+WARM = 8
 CUTS = ((0, 1), (1, 2), (2, KB))
 FLOPS = 2 * K * M * N
 

@@ -72,6 +72,10 @@ def tile_scatter_matmul_kernel(tc, base, x, w, b, offs, out):
         for a in range(MB):
             for k in range(KB // 2, KB):
                 scatter_add(a, k)
-            result = held.tile([P, S], F32, name="result%d" % a)
-            nc.scalar.activation(result[:], window[a][:], TANH, bias=bias[:, a : a + 1])
-            nc.sync.dma_start(out[a * P : (a + 1) * P, :], result[:])
+            pieces = 2 if a == MB - 1 else 1
+            width = S // pieces
+            for i in range(pieces):
+                columns = slice(i * width, (i + 1) * width)
+                result = held.tile([P, width], F32, name="result%d_%d" % (a, i))
+                nc.scalar.activation(result[:], window[a][:, columns], TANH, bias=bias[:, a : a + 1])
+                nc.sync.dma_start(out[a * P : (a + 1) * P, columns], result[:])

@@ -7,6 +7,7 @@ KB = K // P
 MB = M // P
 WARM = 8
 CUTS = ((0, 1), (1, 2), (2, KB))
+HALVES = 2
 FLOPS = 2 * K * M * N
 
 BF16, F32, U16 = mybir.dt.bfloat16, mybir.dt.float32, mybir.dt.uint16
@@ -19,8 +20,11 @@ def tile_scatter_matmul_kernel(tc, base, x, w, b, offs, out):
         tc.tile_pool(name="held", bufs=1) as held,
         tc.psum_pool(name="banks", bufs=1) as banks,
     ):
-        base_sb = held.tile([P, MB, S], BF16, name="base_sb")
-        nc.sync.dma_start(base_sb[:], base.rearrange("(a p) s -> p a s", p=P))
+        base_rows = []
+        for a in range(MB):
+            base_sb = held.tile([P, S], BF16, name="base_sb%d" % a)
+            nc.sync.dma_start(base_sb[:], base[a * P : (a + 1) * P, :])
+            base_rows.append(base_sb)
 
         offsets = held.tile([P, N // 16], U16, name="offsets")
         nc.sync.dma_start(offsets[:], offs)
@@ -54,7 +58,7 @@ def tile_scatter_matmul_kernel(tc, base, x, w, b, offs, out):
 
         window = [banks.tile([P, S], F32, name="window%d" % a) for a in range(MB)]
         for a in range(MB):
-            nc.tensor.matmul(window[a][:], ident[:], base_sb[:, a, :], start=True, stop=False)
+            nc.tensor.matmul(window[a][:], ident[:], base_rows[a][:], start=True, stop=False)
 
         def scatter_add(a, k):
             nc.tensor.matmul(
@@ -72,9 +76,8 @@ def tile_scatter_matmul_kernel(tc, base, x, w, b, offs, out):
         for a in range(MB):
             for k in range(KB // 2, KB):
                 scatter_add(a, k)
-            pieces = 2 if a == MB - 1 else 1
-            width = S // pieces
-            for i in range(pieces):
+            width = S // HALVES
+            for i in range(HALVES):
                 columns = slice(i * width, (i + 1) * width)
                 result = held.tile([P, width], F32, name="result%d_%d" % (a, i))
                 nc.scalar.activation(result[:], window[a][:, columns], TANH, bias=bias[:, a : a + 1])

@@ -5,7 +5,7 @@ P = 128
 S, K, M, N = 512, 512, 256, 512
 KB = K // P
 MB = M // P
-WARM = 8
+WARM = 12
 CUTS = ((0, 1), (1, 2), (2, KB))
 HALVES = 2
 FLOPS = 2 * K * M * N

@@ -6,7 +6,9 @@ S, K, M, N = 512, 512, 256, 512
 KB = K // P
 MB = M // P
 WARM = 12
-CUTS = ((0, 1), (1, 2), (2, KB))
+W_CUTS = ((0, 1), (1, KB))
+X_CUTS = ((1, 2), (2, KB))
+HALF = N // 2
 HALVES = 2
 FLOPS = 2 * K * M * N
 
@@ -32,13 +34,24 @@ def tile_scatter_matmul_kernel(tc, base, x, w, b, offs, out):
         w_rows = w.rearrange("(p k) m -> p k m", k=KB)
         x_rows = x.rearrange("(p k) n -> p k n", k=KB)
         w_block, x_block = {}, {}
-        for first, end in CUTS:
+
+        def load_w(first, end):
             w_sb = held.tile([P, end - first, M], BF16, name="w_sb%d" % first)
             nc.sync.dma_start(w_sb[:], w_rows[:, first:end, :])
+            for k in range(first, end):
+                w_block[k] = w_sb[:, k - first, :]
+
+        load_w(*W_CUTS[0])
+        x_half = []
+        for h in range(2):
+            x_sb = held.tile([P, HALF], BF16, name="x_half%d" % h)
+            nc.sync.dma_start(x_sb[:], x_rows[:, 0, h * HALF : (h + 1) * HALF])
+            x_half.append(x_sb)
+        load_w(*W_CUTS[1])
+        for first, end in X_CUTS:
             x_sb = held.tile([P, end - first, N], BF16, name="x_sb%d" % first)
             nc.sync.dma_start(x_sb[:], x_rows[:, first:end, :])
             for k in range(first, end):
-                w_block[k] = w_sb[:, k - first, :]
                 x_block[k] = x_sb[:, k - first, :]
 
         bias = held.tile([P, MB], F32, name="bias")
@@ -69,9 +82,18 @@ def tile_scatter_matmul_kernel(tc, base, x, w, b, offs, out):
                 stop=(k == KB - 1),
             )
 
-        for k in range(KB // 2):
+        for h in range(2):
             for a in range(MB):
-                scatter_add(a, k)
+                nc.tensor.matmul(
+                    window[a][:].indirect(offsets[:, h * HALF // 16 : (h + 1) * HALF // 16]),
+                    w_block[0][:, a * P : (a + 1) * P],
+                    x_half[h][:],
+                    start=False,
+                    stop=False,
+                )
+
+        for a in range(MB):
+            scatter_add(a, 1)
 
         for a in range(MB):
             for k in range(KB // 2, KB):

@@ -6,8 +6,6 @@ S, K, M, N = 512, 512, 256, 512
 KB = K // P
 MB = M // P
 WARM = 12
-W_CUTS = ((0, 1), (1, KB))
-X_CUTS = ((1, 2), (2, KB))
 HALF = N // 2
 HALVES = 2
 FLOPS = 2 * K * M * N
@@ -33,26 +31,17 @@ def tile_scatter_matmul_kernel(tc, base, x, w, b, offs, out):
 
         w_rows = w.rearrange("(p k) m -> p k m", k=KB)
         x_rows = x.rearrange("(p k) n -> p k n", k=KB)
-        w_block, x_block = {}, {}
+        w_sb = held.tile([P, KB, M], BF16, name="w_sb")
+        x_sb = [held.tile([P, N], BF16, name="x_sb%d" % k) for k in range(KB)]
 
-        def load_w(first, end):
-            w_sb = held.tile([P, end - first, M], BF16, name="w_sb%d" % first)
-            nc.sync.dma_start(w_sb[:], w_rows[:, first:end, :])
-            for k in range(first, end):
-                w_block[k] = w_sb[:, k - first, :]
-
-        load_w(*W_CUTS[0])
-        x_half = []
+        nc.sync.dma_start(w_sb[:, 0, 0:P], w_rows[:, 0, 0:P])
         for h in range(2):
-            x_sb = held.tile([P, HALF], BF16, name="x_half%d" % h)
-            nc.sync.dma_start(x_sb[:], x_rows[:, 0, h * HALF : (h + 1) * HALF])
-            x_half.append(x_sb)
-        load_w(*W_CUTS[1])
-        for first, end in X_CUTS:
-            x_sb = held.tile([P, end - first, N], BF16, name="x_sb%d" % first)
-            nc.sync.dma_start(x_sb[:], x_rows[:, first:end, :])
-            for k in range(first, end):
-                x_block[k] = x_sb[:, k - first, :]
+            columns = slice(h * HALF, (h + 1) * HALF)
+            nc.sync.dma_start(x_sb[0][:, columns], x_rows[:, 0, columns])
+        nc.sync.dma_start(w_sb[:, 0, P:M], w_rows[:, 0, P:M])
+        nc.sync.dma_start(w_sb[:, 1:KB, :], w_rows[:, 1:KB, :])
+        for k in range(1, KB):
+            nc.sync.dma_start(x_sb[k][:], x_rows[:, k, :])
 
         bias = held.tile([P, MB], F32, name="bias")
         nc.sync.dma_start(bias[:], b.rearrange("(a p) o -> p (a o)", p=P))
@@ -73,24 +62,18 @@ def tile_scatter_matmul_kernel(tc, base, x, w, b, offs, out):
         for a in range(MB):
             nc.tensor.matmul(window[a][:], ident[:], base_rows[a][:], start=True, stop=False)
 
-        def scatter_add(a, k):
+        def scatter_add(a, k, first=0, end=N):
             nc.tensor.matmul(
-                window[a][:].indirect(offsets[:]),
-                w_block[k][:, a * P : (a + 1) * P],
-                x_block[k],
+                window[a][:].indirect(offsets[:, first // 16 : end // 16]),
+                w_sb[:, k, a * P : (a + 1) * P],
+                x_sb[k][:, first:end],
                 start=False,
                 stop=(k == KB - 1),
             )
 
         for h in range(2):
-            for a in range(MB):
-                nc.tensor.matmul(
-                    window[a][:].indirect(offsets[:, h * HALF // 16 : (h + 1) * HALF // 16]),
-                    w_block[0][:, a * P : (a + 1) * P],
-                    x_half[h][:],
-                    start=False,
-                    stop=False,
-                )
+            scatter_add(0, 0, h * HALF, (h + 1) * HALF)
+        scatter_add(1, 0)
 
         for a in range(MB):
             scatter_add(a, 1)

@@ -6,6 +6,7 @@ S, K, M, N = 512, 512, 256, 512
 KB = K // P
 MB = M // P
 WARM = 12
+ALIGN = 256
 HALF = N // 2
 HALVES = 2
 FLOPS = 2 * K * M * N
@@ -22,17 +23,17 @@ def tile_scatter_matmul_kernel(tc, base, x, w, b, offs, out):
     ):
         base_rows = []
         for a in range(MB):
-            base_sb = held.tile([P, S], BF16, name="base_sb%d" % a)
+            base_sb = held.tile([P, S], BF16, name="base_sb%d" % a, align_bytes=ALIGN)
             nc.sync.dma_start(base_sb[:], base[a * P : (a + 1) * P, :])
             base_rows.append(base_sb)
 
-        offsets = held.tile([P, N // 16], U16, name="offsets")
+        offsets = held.tile([P, N // 16], U16, name="offsets", align_bytes=ALIGN)
         nc.sync.dma_start(offsets[:], offs)
 
         w_rows = w.rearrange("(p k) m -> p k m", k=KB)
         x_rows = x.rearrange("(p k) n -> p k n", k=KB)
-        w_sb = held.tile([P, KB, M], BF16, name="w_sb")
-        x_sb = [held.tile([P, N], BF16, name="x_sb%d" % k) for k in range(KB)]
+        w_sb = held.tile([P, KB, M], BF16, name="w_sb", align_bytes=ALIGN)
+        x_sb = [held.tile([P, N], BF16, name="x_sb%d" % k, align_bytes=ALIGN) for k in range(KB)]
 
         nc.sync.dma_start(w_sb[:, 0, 0:P], w_rows[:, 0, 0:P])
         for h in range(2):
@@ -84,6 +85,6 @@ def tile_scatter_matmul_kernel(tc, base, x, w, b, offs, out):
             width = S // HALVES
             for i in range(HALVES):
                 columns = slice(i * width, (i + 1) * width)
-                result = held.tile([P, width], F32, name="result%d_%d" % (a, i))
+                result = held.tile([P, width], F32, name="result%d_%d" % (a, i), align_bytes=ALIGN)
                 nc.scalar.activation(result[:], window[a][:, columns], TANH, bias=bias[:, a : a + 1])
                 nc.sync.dma_start(out[a * P : (a + 1) * P, columns], result[:])

@@ -5,7 +5,7 @@ P = 128
 S, K, M, N = 512, 512, 256, 512
 KB = K // P
 MB = M // P
-WARM = 12
+WARM = 8
 ALIGN = 256
 HALF = N // 2
 HALVES = 2

import concourse.mybir as mybir
from concourse.masks import make_identity

P = 128
S, K, M, N = 512, 512, 256, 512
KB = K // P
MB = M // P
WARM = 8
ALIGN = 256
HALF = N // 2
HALVES = 2
FLOPS = 2 * K * M * N

BF16, F32, U16 = mybir.dt.bfloat16, mybir.dt.float32, mybir.dt.uint16
TANH = mybir.ActivationFunctionType.Tanh


def tile_scatter_matmul_kernel(tc, base, x, w, b, offs, out):
    nc = tc.nc
    with (
        tc.tile_pool(name="held", bufs=1) as held,
        tc.psum_pool(name="banks", bufs=1) as banks,
    ):
        base_rows = []
        for a in range(MB):
            base_sb = held.tile([P, S], BF16, name="base_sb%d" % a, align_bytes=ALIGN)
            nc.sync.dma_start(base_sb[:], base[a * P : (a + 1) * P, :])
            base_rows.append(base_sb)

        offsets = held.tile([P, N // 16], U16, name="offsets", align_bytes=ALIGN)
        nc.sync.dma_start(offsets[:], offs)

        w_rows = w.rearrange("(p k) m -> p k m", k=KB)
        x_rows = x.rearrange("(p k) n -> p k n", k=KB)
        w_sb = held.tile([P, KB, M], BF16, name="w_sb", align_bytes=ALIGN)
        x_sb = [held.tile([P, N], BF16, name="x_sb%d" % k, align_bytes=ALIGN) for k in range(KB)]

        nc.sync.dma_start(w_sb[:, 0, 0:P], w_rows[:, 0, 0:P])
        for h in range(2):
            columns = slice(h * HALF, (h + 1) * HALF)
            nc.sync.dma_start(x_sb[0][:, columns], x_rows[:, 0, columns])
        nc.sync.dma_start(w_sb[:, 0, P:M], w_rows[:, 0, P:M])
        nc.sync.dma_start(w_sb[:, 1:KB, :], w_rows[:, 1:KB, :])
        for k in range(1, KB):
            nc.sync.dma_start(x_sb[k][:], x_rows[:, k, :])

        bias = held.tile([P, MB], F32, name="bias")
        nc.sync.dma_start(bias[:], b.rearrange("(a p) o -> p (a o)", p=P))

        zeros = held.tile([P, P], BF16, name="zeros")
        nc.gpsimd.memset(zeros[:], 0.0)
        idle_bank = banks.tile([P, P], F32, name="idle_bank")
        for i in range(WARM):
            nc.tensor.matmul(idle_bank[:], zeros[:], zeros[:], start=True, stop=True)

        early_tanh = held.tile([P, 1], F32, name="early_tanh")
        nc.scalar.activation(early_tanh[:], zeros[:, 0:1], TANH)

        ident = held.tile([P, P], BF16, name="ident")
        make_identity(nc, ident[:])

        window = [banks.tile([P, S], F32, name="window%d" % a) for a in range(MB)]
        for a in range(MB):
            nc.tensor.matmul(window[a][:], ident[:], base_rows[a][:], start=True, stop=False)

        def scatter_add(a, k, first=0, end=N):
            nc.tensor.matmul(
                window[a][:].indirect(offsets[:, first // 16 : end // 16]),
                w_sb[:, k, a * P : (a + 1) * P],
                x_sb[k][:, first:end],
                start=False,
                stop=(k == KB - 1),
            )

        for h in range(2):
            scatter_add(0, 0, h * HALF, (h + 1) * HALF)
        scatter_add(1, 0)

        for a in range(MB):
            scatter_add(a, 1)

        for a in range(MB):
            for k in range(KB // 2, KB):
                scatter_add(a, k)
            width = S // HALVES
            for i in range(HALVES):
                columns = slice(i * width, (i + 1) * width)
                result = held.tile([P, width], F32, name="result%d_%d" % (a, i), align_bytes=ALIGN)
                nc.scalar.activation(result[:], window[a][:, columns], TANH, bias=bias[:, a : a + 1])
                nc.sync.dma_start(out[a * P : (a + 1) * P, columns], result[:])
